import numpy as np
import ml_dtypes


def mxq(x, axis, fmt="e4m3"):
    dtype, down = {"e4m3": (ml_dtypes.float8_e4m3fn, 7), "e5m2": (ml_dtypes.float8_e5m2, 14)}[fmt]
    v = np.moveaxis(np.asarray(x, np.float32).astype(ml_dtypes.bfloat16).astype(np.float64), axis, -1)
    blocks = v.reshape(v.shape[:-1] + (-1, 32))
    amax = np.abs(blocks).max(-1, keepdims=True)
    byte = np.maximum(np.where(amax > 0, np.frexp(amax)[1] - 1 + 127, 0) - down, 1)
    scale = np.exp2(byte - 127.0)
    codes = (blocks / scale).astype(np.float32).astype(dtype).astype(np.float64)
    return np.moveaxis((codes * scale).reshape(v.shape), -1, axis)


WIDE = False


def mx_kscale(k):
    if not WIDE:
        return np.ones(k)
    levels = np.array([10, -10, 5, -5, 0])
    if k % 512:
        return np.exp2(np.random.permutation(np.resize(levels, k // 32))).repeat(32)
    a = np.empty((k // 512, 16))
    for p in range(k // 512):
        a[p, :8] = np.random.permutation(np.resize(levels, 8))
        for g in range(8):
            far = levels[np.abs(levels - a[p, g]) >= 10]
            a[p, g + 8] = far[np.random.randint(len(far))]
    return np.exp2(a.ravel()).repeat(32)


def f64(x):
    return np.asarray(x).astype(np.float64)


def striped(idx):
    return np.tile(idx.reshape(-1, 16).T, (8, 1)).astype(np.uint16)


def unstriped(offs):
    return offs[:16].T.reshape(-1).astype(np.int64)


def pack_weight(w):
    k, n = w.shape
    w = f64(np.asarray(w, np.float32).astype(ml_dtypes.bfloat16)).reshape(k // 32, 32, n)
    amax = np.abs(w).max(1)
    byte = np.clip(np.where(amax > 0, np.frexp(amax)[1] - 1 + 127 - 7, 1), 1, 254)
    scaled = (w * np.exp2(127.0 - byte)[:, None, :]).reshape(k, n).astype(np.float32)
    words = np.ascontiguousarray(scaled.reshape(k // 512, 128, 4, n).transpose(0, 1, 3, 2)).astype(ml_dtypes.float8_e4m3fn).view(np.uint8)
    return words, np.ascontiguousarray(byte.astype(np.uint8).reshape(k // 512, 16, n))


def unpack_weight(words, scales):
    g, p, n, _ = words.shape
    vals = np.ascontiguousarray(words).view(ml_dtypes.float8_e4m3fn).astype(np.float64) * np.repeat(np.exp2(scales.astype(np.float64) - 127.0), 8, axis=1)[..., None]
    return vals.transpose(0, 1, 3, 2).reshape(g * 512, n)


E2M1 = np.array([0.0, 0.5, 1.0, 1.5, 2.0, 3.0, 4.0, 6.0, -0.0, -0.5, -1.0, -1.5, -2.0, -3.0, -4.0, -6.0])


def pack_fp4(w):
    k, n = w.shape
    w = f64(np.asarray(w, np.float32).astype(ml_dtypes.bfloat16)).reshape(k // 32, 32, n)
    amax = np.abs(w).max(1)
    mant, ex = np.frexp(amax / 6.0)
    byte = np.clip(np.where(amax > 0, np.where(mant > 0.5, ex, ex - 1) + 127, 1), 1, 254)
    scaled = (w * np.exp2(127.0 - byte)[:, None, :]).reshape(k, n).astype(np.float32)
    c = np.ascontiguousarray(scaled.reshape(k // 512, 128, 4, n).transpose(0, 1, 3, 2)).astype(ml_dtypes.float4_e2m1fn).view(np.uint8) & 0xF
    words = (c[..., 0::2] | (c[..., 1::2] << 4)).reshape(k // 512, 128, 2 * n)
    return np.ascontiguousarray(words), np.ascontiguousarray(byte.astype(np.uint8).reshape(k // 512, 16, n))


def unpack_fp4(words, scales):
    g, _, n = scales.shape
    words = np.ascontiguousarray(words).reshape(g, 128, n, 2)
    nib = np.empty((g, 128, n, 4), np.uint8)
    nib[..., 0::2] = words & 0xF
    nib[..., 1::2] = words >> 4
    vals = E2M1[nib] * np.repeat(np.exp2(scales.astype(np.float64) - 127.0), 8, axis=1)[..., None]
    return vals.transpose(0, 1, 3, 2).reshape(g * 512, n)


def sigmoid(v):
    return 1.0 / (1.0 + np.exp(-np.maximum(v, -700.0)))

def planes(y):
    n, m = y.shape
    v = y.astype(np.float32).astype(ml_dtypes.bfloat16).astype(np.float64).reshape(n // 32, 32, m)
    top = np.abs(v).max(1)
    byte = np.clip(np.where(top > 0, np.frexp(top)[1] - 1 + 127 - 7, 1), 1, 254)
    codes = (v * np.exp2(127.0 - byte)[:, None, :]).reshape(n, m).astype(np.float32).astype(ml_dtypes.float8_e4m3fn).view(np.uint8)
    words = codes.reshape(n // 512, 128, 4, m).transpose(0, 1, 3, 2)
    return np.ascontiguousarray(words), np.ascontiguousarray(byte.astype(np.uint8).reshape(n // 512, 16, m))


K, T, S, H, C = 512, 2048, 512, 512, 512


def setup_inputs():
    n = np.random.standard_normal
    s = mx_kscale(K)[:, None]
    packed_xT = pack_weight(n((K, T)) * s)
    packed_w1 = pack_fp4(n((K, H)) / np.sqrt(K) / s)
    return {
        "x_words": packed_xT[0],
        "x_scales": packed_xT[1],
        "w1_words": packed_w1[0],
        "w1_scales": packed_w1[1],
        "sl": np.random.uniform(1.0, 2.0, (H, 1)).astype(np.float32),
        "th": (0.5 * n((H, 1))).astype(np.float32),
        "gs": (np.random.uniform(0.5, 1.5, (K, 1)) / s).astype(np.float32),
        "wb": (n((K, S)) / np.sqrt(K) / s).astype(np.float32),
        "sl2": np.random.uniform(1.0, 2.0, (C, 1)).astype(np.float32),
        "th2": (0.5 * n((C, 1))).astype(np.float32),
        "offs": striped(np.random.permutation(T)[:S]),
        "n1": striped(np.random.permutation(S)),
        "n2": striped(np.random.permutation(S)),
        "n3": striped(np.random.permutation(S)),
        "cand": striped(np.random.permutation(T)[:C]),
        "cb": striped(np.random.permutation(T)[:C]),
        "n4": striped(np.random.permutation(S)),
        "n5": striped(np.random.permutation(S)),
    }


def reference(x_words, x_scales, w1_words, w1_scales, sl, th, gs, wb, sl2, th2, offs, n1, n2, n3, cand, cb, n4, n5):
    x_cand = unpack_weight(x_words, x_scales)[:, unstriped(cand)]
    xq = unpack_weight(x_words, x_scales)[:, unstriped(offs)]
    y = unpack_fp4(w1_words, w1_scales).T @ xq
    own = sigmoid(f64(sl) * (y - f64(th)))
    sg = sigmoid(f64(sl) * (y[:, unstriped(n1)] - f64(th)))
    z = f64(gs) * (y[:, unstriped(n2)] * own + y[:, unstriped(n3)] * sg)
    a = 0.0625 * ((x_cand.T @ mxq(z, 0, "e4m3")))
    x_cb = unpack_weight(x_words, x_scales)[:, unstriped(cb)]
    b = x_cb.T @ mxq(f64(wb), 0, "e4m3")
    sg2 = sigmoid(f64(sl2) * (b[:, unstriped(n4)] - f64(th2)))
    out_0 = np.maximum(a * sg2, b[:, unstriped(n5)] - b)
    return (out_0,) + planes(out_0)

@@ -1,0 +1,275 @@
+from contextlib import ExitStack
+
+import concourse.mybir as mybir
+
+K, T, S = 512, 2048, 512
+FLOPS = 3 * 2 * K * S * S
+
+F32 = mybir.dt.float32
+BF16 = mybir.dt.bfloat16
+I32 = mybir.dt.int32
+U32 = mybir.dt.uint32
+U16 = mybir.dt.uint16
+U8 = mybir.dt.uint8
+FP8X4 = mybir.dt.float8_e4m3fn_x4
+FP4X4 = mybir.dt.float4_e2m1fn_x4
+ALU = mybir.AluOpType
+ACT = mybir.ActivationFunctionType
+
+P = 128
+PACK = 4
+HALF = S // 2
+LIST_COLS = S // 16
+
+
+def tile_picked_cdswmxbemx_none_po_kernel(
+    tc, x_words, x_scales, w1_words, w1_scales, sl, th, gs, wb, sl2, th2, offs, n1, n2, n3, cand, cb, n4, n5, out_0, out_1, out_2
+):
+    nc = tc.nc
+    with ExitStack() as ctx:
+        lists = ctx.enter_context(tc.tile_pool(name="lists", bufs=1))
+        sb = ctx.enter_context(tc.tile_pool(name="sb", bufs=1))
+        psum = ctx.enter_context(tc.psum_pool(name="psum", bufs=1))
+
+        def new(name, shape, dtype):
+            return sb.tile(shape, dtype, name=name, align_bytes=64)
+
+        def load_list(name, src):
+            t = lists.tile([P, LIST_COLS], U16, name=name)
+            nc.sync.dma_start(t[:], src)
+            return t
+
+        def load_rows(name, src, queue):
+            t = new(name, [P, PACK], F32)
+            queue.dma_start(t[:], src.rearrange("(p t) o -> p (t o)", t=PACK))
+            return t
+
+        def load_scale_rows(dst, src, queues):
+            for q in range(4):
+                queues[q].dma_start(dst[32 * q : 32 * q + 4, :].bitcast(I32), src[4 * q : 4 * q + 4, :].bitcast(I32))
+
+        def half_cols(h):
+            return slice(h * HALF, (h + 1) * HALF)
+
+        def half_list(lst, h):
+            return lst[:, h * LIST_COLS // 2 : (h + 1) * LIST_COLS // 2]
+
+        def woven(t):
+            return t.rearrange("p (c i) t -> p c t i", i=4)
+
+        def planar(t):
+            return t.rearrange("p t (c i) -> p c t i", i=4)
+
+        def dealt(t):
+            return t.rearrange("p (t m) -> p m t", t=PACK)
+
+        xs = new("xs", [P, T], U8)
+        nc.gpsimd.memset(xs[:].bitcast(I32), 0)
+        w1s = new("w1s", [P, S], U8)
+        nc.gpsimd.memset(w1s[:].bitcast(I32), 0)
+
+        l_offs = load_list("l_offs", offs)
+        xw = new("xw", [P, T], U32)
+        nc.sync.dma_start(xw[:].bitcast(I32), x_words[0].rearrange("p n t -> p (n t)").bitcast(I32))
+        w1w = new("w1w", [P, 2 * S], U8)
+        nc.scalar.dma_start(w1w[:].bitcast(I32), w1_words[0].bitcast(I32))
+        load_scale_rows(xs, x_scales[0], [nc.scalar] * 4)
+        load_scale_rows(w1s, w1_scales[0], [nc.scalar, nc.scalar, nc.gpsimd, nc.gpsimd])
+        sl_t = load_rows("sl_t", sl, nc.sync)
+        th_t = load_rows("th_t", th, nc.sync)
+        l_cb = load_list("l_cb", cb)
+        l_n1 = load_list("l_n1", n1)
+        l_n2 = load_list("l_n2", n2)
+        l_cand = load_list("l_cand", cand)
+        wb_raw = new("wb_raw", [P, PACK, S], F32)
+        nc.sync.dma_start(wb_raw[:], wb.rearrange("(p t) n -> p t n", t=PACK))
+        l_n3 = load_list("l_n3", n3)
+        gs_t = load_rows("gs_t", gs, nc.sync)
+        sl2_t = load_rows("sl2_t", sl2, nc.sync)
+        th2_t = load_rows("th2_t", th2, nc.sync)
+        l_n4 = load_list("l_n4", n4)
+        l_n5 = load_list("l_n5", n5)
+
+        w1w_d = new("w1w_d", [P, 2 * S], U8)
+        nc.scalar.copy(
+            w1w_d[:].bitcast(U16).rearrange("p (t m) -> p t m", t=PACK),
+            w1w[:].bitcast(U16).rearrange("p (m t) -> p t m", t=PACK),
+        )
+        xq_s = new("xq_s", [P, S], U8)
+        nc.vector.tensor_copy(xq_s[:], xs[:].indirect(l_offs[:]))
+        w1s_d = new("w1s_d", [P, S], U8)
+        nc.vector.tensor_copy(
+            w1s_d[:].rearrange("p (t m) -> p t m", t=PACK), w1s[:].rearrange("p (m t) -> p t m", t=PACK)
+        )
+        xq_w = new("xq_w", [P, S], U32)
+        nc.vector.tensor_copy(xq_w[:], xw[:].indirect(l_offs[:]))
+        bias = new("bias", [P, PACK], F32)
+        nc.vector.scalar_tensor_tensor(bias[:], sl_t[:], -1.0, th_t[:], ALU.mult, ALU.mult)
+
+        y_ps = [psum.tile([P, S], F32, name=f"y_ps{t}", tag=f"ya{t}") for t in range(PACK)]
+        for t in range(PACK):
+            nc.tensor.matmul_mx(
+                y_ps[t][:],
+                lhsT=w1w_d[:, 2 * P * t : 2 * P * (t + 1)].bitcast(FP4X4),
+                lhsT_scale=w1s_d[:, P * t : P * (t + 1)],
+                rhs=xq_w[:].bitcast(FP8X4),
+                rhs_scale=xq_s[:],
+                start=True,
+                stop=True,
+            )
+
+        def pick(name, lst):
+            words = new(name + "_w", [P, S], U32)
+            scales = new(name + "_s", [P, S], U8)
+            nc.vector.tensor_copy(dealt(words[:]), xw[:].indirect(lst[:]))
+            nc.vector.tensor_copy(dealt(scales[:]), xs[:].indirect(lst[:]))
+            return words, scales
+
+        cb_w, cb_s = pick("cb", l_cb)
+        cand_w, cand_s = pick("cand", l_cand)
+
+        wb_bf = new("wb_bf", [P, S, PACK], BF16)
+        for c in range(4):
+            cols = slice(c * P, (c + 1) * P)
+            nc.gpsimd.tensor_scalar(woven(wb_bf[:, cols, :]), planar(wb_raw[:, :, cols]), 1.0, 0.0, ALU.mult, ALU.add)
+
+        def halves(name, dtype=F32):
+            return [new(f"{name}{h}", [P, PACK, HALF], dtype) for h in range(2)]
+
+        y_sb = [new(f"y_sb{t}", [P, S], F32) for t in range(PACK)]
+        b_sb = [new(f"b_sb{t}", [P, S], F32) for t in range(PACK)]
+        own = [new(f"own{t}", [P, S], F32) for t in range(PACK)]
+        sg, y2, y3, u, v = halves("sg"), halves("y2"), halves("y3"), halves("u"), halves("v")
+
+        def fetch_y(t, h):
+            col = slice(t, t + 1)
+            nc.scalar.activation(
+                sg[h][:, t, :], y_sb[t][:].indirect(half_list(l_n1, h)), ACT.Sigmoid, bias=bias[:, col], scale=sl_t[:, col]
+            )
+            nc.scalar.activation(y2[h][:, t, :], y_sb[t][:].indirect(half_list(l_n2, h)), ACT.Copy)
+
+        def fetch_y3(t, h):
+            nc.vector.tensor_copy(y3[h][:, t, :], y_sb[t][:].indirect(half_list(l_n3, h)))
+
+        def terms(t, h):
+            col = slice(t, t + 1)
+            nc.vector.scalar_tensor_tensor(u[h][:, t, :], y3[h][:, t, :], gs_t[:, col], sg[h][:, t, :], ALU.mult, ALU.mult)
+            nc.vector.scalar_tensor_tensor(
+                v[h][:, t, :], y2[h][:, t, :], gs_t[:, col], own[t][:, half_cols(h)], ALU.mult, ALU.mult
+            )
+
+        z_bf = [new(f"z_bf{h}", [P, HALF, PACK], BF16) for h in range(2)]
+        z_w = [new(f"z_w{h}", [P, HALF], U32) for h in range(2)]
+        z_s = [new(f"z_s{h}", [P, HALF], U8) for h in range(2)]
+        a_ps = {}
+
+        def z_sum(h):
+            nc.vector.tensor_tensor(woven(z_bf[h][:]), planar(u[h][:]), planar(v[h][:]), ALU.add)
+
+        def z_product(h):
+            nc.vector.quantize_mx(z_w[h][:].bitcast(FP8X4), z_s[h][:], z_bf[h][:].rearrange("p n t -> p (n t)"))
+            for pair in range(2):
+                bank = psum.tile([P, 2, HALF], F32, name=f"a_ps{h}{pair}", tag=f"ya{2 * h + pair}")
+                a_ps[h, pair] = bank
+                for i in range(2):
+                    t = 2 * pair + i
+                    nc.tensor.matmul_mx(
+                        bank[:, i, :],
+                        lhsT=cand_w[:, P * t : P * (t + 1)].bitcast(FP8X4),
+                        lhsT_scale=cand_s[:, P * t : P * (t + 1)],
+                        rhs=z_w[h][:].bitcast(FP8X4),
+                        rhs_scale=z_s[h][:],
+                        start=True,
+                        stop=True,
+                    )
+
+        def open_y(t):
+            col = slice(t, t + 1)
+            nc.scalar.activation(own[t][:], y_ps[t][:], ACT.Sigmoid, bias=bias[:, col], scale=sl_t[:, col])
+            nc.scalar.copy(y_sb[t][:], y_ps[t][:])
+
+        for t in range(PACK):
+            open_y(t)
+            fetch_y(t, 0)
+
+        fetch_y3(0, 0)
+        fetch_y3(1, 0)
+        terms(0, 0)
+        wb_w = new("wb_w", [P, S], U32)
+        wb_s = new("wb_s", [P, S], U8)
+        nc.vector.quantize_mx(wb_w[:].bitcast(FP8X4), wb_s[:], wb_bf[:].rearrange("p n t -> p (n t)"))
+        b_ps = [psum.tile([P, S], F32, name=f"b_ps{t}", tag=f"b{t}") for t in range(PACK)]
+        for t in range(PACK):
+            nc.tensor.matmul_mx(
+                b_ps[t][:],
+                lhsT=cb_w[:, P * t : P * (t + 1)].bitcast(FP8X4),
+                lhsT_scale=cb_s[:, P * t : P * (t + 1)],
+                rhs=wb_w[:].bitcast(FP8X4),
+                rhs_scale=wb_s[:],
+                start=True,
+                stop=True,
+            )
+        bias2 = new("bias2", [P, PACK], F32)
+        nc.vector.scalar_tensor_tensor(bias2[:], sl2_t[:], -1.0, th2_t[:], ALU.mult, ALU.mult)
+        terms(1, 0)
+        fetch_y3(0, 1)
+        fetch_y3(1, 1)
+        fetch_y3(2, 0)
+        terms(2, 0)
+        fetch_y3(2, 1)
+        fetch_y3(3, 0)
+        terms(3, 0)
+        fetch_y3(3, 1)
+        for t in range(PACK):
+            fetch_y(t, 1)
+        z_sum(0)
+        nc.vector.tensor_copy(b_sb[0][:], b_ps[0][:])
+        z_product(0)
+        nc.vector.tensor_copy(b_sb[1][:], b_ps[1][:])
+        for t in range(PACK):
+            terms(t, 1)
+        nc.scalar.copy(b_sb[2][:], b_ps[2][:])
+        nc.scalar.copy(b_sb[3][:], b_ps[3][:])
+        z_sum(1)
+
+        sg2, b5, q, dd, res = halves("sg2"), halves("b5"), halves("q"), halves("dd"), halves("res")
+        res_bf = [new(f"res_bf{h}", [P, HALF, PACK], BF16) for h in range(2)]
+        res_w = new("res_w", [P, S], U32)
+        res_s = new("res_s", [P, S], U8)
+        out_rows = out_0.rearrange("(p t) j -> p t j", t=PACK)
+        out_words = out_1[0].rearrange("p n t -> p (n t)").bitcast(I32)
+
+        def fetch_b(t, h):
+            col = slice(t, t + 1)
+            nc.scalar.activation(
+                sg2[h][:, t, :], b_sb[t][:].indirect(half_list(l_n4, h)), ACT.Sigmoid, bias=bias2[:, col], scale=sl2_t[:, col]
+            )
+            nc.scalar.activation(b5[h][:, t, :], b_sb[t][:].indirect(half_list(l_n5, h)), ACT.Copy)
+
+        def finish_pair(h, pair):
+            ts = slice(2 * pair, 2 * pair + 2)
+            t0, t1 = 2 * pair, 2 * pair + 1
+            nc.vector.tensor_tensor(dd[h][:, t0, :], b5[h][:, t0, :], b_sb[t0][:, half_cols(h)], ALU.subtract)
+            nc.vector.scalar_tensor_tensor(q[h][:, ts, :], a_ps[h, pair][:], 0.0625, sg2[h][:, ts, :], ALU.mult, ALU.mult)
+            nc.vector.tensor_tensor(dd[h][:, t1, :], b5[h][:, t1, :], b_sb[t1][:, half_cols(h)], ALU.subtract)
+            nc.vector.tensor_tensor(res[h][:, ts, :], q[h][:, ts, :], dd[h][:, ts, :], ALU.max)
+            nc.sync.dma_start(out_rows[:, ts, half_cols(h)], res[h][:, ts, :])
+
+        def planes(h):
+            nc.vector.tensor_copy(woven(res_bf[h][:]), planar(res[h][:]))
+            nc.vector.quantize_mx(
+                res_w[:, half_cols(h)].bitcast(FP8X4), res_s[:, half_cols(h)], res_bf[h][:].rearrange("p n t -> p (n t)")
+            )
+            nc.sync.dma_start(out_words[:, half_cols(h)], res_w[:, half_cols(h)].bitcast(I32))
+
+        for h in range(2):
+            for t in range(PACK):
+                fetch_b(t, h)
+        z_product(1)
+        for h in range(2):
+            finish_pair(h, 0)
+            finish_pair(h, 1)
+            planes(h)
+        for qd in range(4):
+            queue = nc.scalar if qd % 2 else nc.sync
+            queue.dma_start(out_2[0][4 * qd : 4 * qd + 4, :].bitcast(I32), res_s[32 * qd : 32 * qd + 4, :].bitcast(I32))

@@ -60,9 +60,6 @@ def tile_picked_cdswmxbemx_none_po_kernel(
         def planar(t):
             return t.rearrange("p t (c i) -> p c t i", i=4)
 
-        def dealt(t):
-            return t.rearrange("p (t m) -> p m t", t=PACK)
-
         xs = new("xs", [P, T], U8)
         nc.gpsimd.memset(xs[:].bitcast(I32), 0)
         w1s = new("w1s", [P, S], U8)
@@ -103,8 +100,15 @@ def tile_picked_cdswmxbemx_none_po_kernel(
         )
         xq_w = new("xq_w", [P, S], U32)
         nc.vector.tensor_copy(xq_w[:], xw[:].indirect(l_offs[:]))
-        bias = new("bias", [P, PACK], F32)
-        nc.vector.scalar_tensor_tensor(bias[:], sl_t[:], -1.0, th_t[:], ALU.mult, ALU.mult)
+
+        def neg_product(name, slope, threshold):
+            prod = new(name + "_prod", [P, PACK], F32)
+            neg = new(name, [P, PACK], F32)
+            nc.gpsimd.tensor_tensor(prod[:], slope[:], threshold[:], ALU.mult)
+            nc.gpsimd.tensor_scalar(neg[:], prod[:], -1.0, 0.0, ALU.mult, ALU.add)
+            return neg
+
+        bias = neg_product("bias", sl_t, th_t)
 
         y_ps = [psum.tile([P, S], F32, name=f"y_ps{t}", tag=f"ya{t}") for t in range(PACK)]
         for t in range(PACK):
@@ -118,20 +122,33 @@ def tile_picked_cdswmxbemx_none_po_kernel(
                 stop=True,
             )
 
-        def pick(name, lst):
-            words = new(name + "_w", [P, S], U32)
-            scales = new(name + "_s", [P, S], U8)
-            nc.vector.tensor_copy(dealt(words[:]), xw[:].indirect(lst[:]))
-            nc.vector.tensor_copy(dealt(scales[:]), xs[:].indirect(lst[:]))
-            return words, scales
+        def gather(name, window, lst, dtype):
+            t = new(name, [P, S], dtype)
+            nc.vector.tensor_copy(t[:], window[:].indirect(lst[:]))
+            return t
 
-        cb_w, cb_s = pick("cb", l_cb)
-        cand_w, cand_s = pick("cand", l_cand)
+        def deal(name, src, dtype, run):
+            t = new(name, [P, S], dtype)
+            nc.vector.tensor_copy(
+                t[:].rearrange("p (t c i) -> p c t i", t=PACK, i=run),
+                src[:].rearrange("p (c i t) -> p c t i", t=PACK, i=run),
+            )
+            return t
+
+        cb_w0 = gather("cb_w0", xw, l_cb, U32)
+        cb_s0 = gather("cb_s0", xs, l_cb, U8)
+        cb_w = deal("cb_w", cb_w0, U32, 4)
+        cand_w0 = gather("cand_w0", xw, l_cand, U32)
+        cb_s = deal("cb_s", cb_s0, U8, 16)
+        cand_s0 = gather("cand_s0", xs, l_cand, U8)
+        cand_w = deal("cand_w", cand_w0, U32, 4)
 
         wb_bf = new("wb_bf", [P, S, PACK], BF16)
         for c in range(4):
             cols = slice(c * P, (c + 1) * P)
             nc.gpsimd.tensor_scalar(woven(wb_bf[:, cols, :]), planar(wb_raw[:, :, cols]), 1.0, 0.0, ALU.mult, ALU.add)
+
+        bias2 = neg_product("bias2", sl2_t, th2_t)
 
         def halves(name, dtype=F32):
             return [new(f"{name}{h}", [P, PACK, HALF], dtype) for h in range(2)]
@@ -141,11 +158,13 @@ def tile_picked_cdswmxbemx_none_po_kernel(
         own = [new(f"own{t}", [P, S], F32) for t in range(PACK)]
         sg, y2, y3, u, v = halves("sg"), halves("y2"), halves("y3"), halves("u"), halves("v")
 
-        def fetch_y(t, h):
+        def fetch_sg(t, h):
             col = slice(t, t + 1)
             nc.scalar.activation(
                 sg[h][:, t, :], y_sb[t][:].indirect(half_list(l_n1, h)), ACT.Sigmoid, bias=bias[:, col], scale=sl_t[:, col]
             )
+
+        def fetch_y2(t, h):
             nc.scalar.activation(y2[h][:, t, :], y_sb[t][:].indirect(half_list(l_n2, h)), ACT.Copy)
 
         def fetch_y3(t, h):
@@ -153,10 +172,10 @@ def tile_picked_cdswmxbemx_none_po_kernel(
 
         def terms(t, h):
             col = slice(t, t + 1)
-            nc.vector.scalar_tensor_tensor(u[h][:, t, :], y3[h][:, t, :], gs_t[:, col], sg[h][:, t, :], ALU.mult, ALU.mult)
             nc.vector.scalar_tensor_tensor(
                 v[h][:, t, :], y2[h][:, t, :], gs_t[:, col], own[t][:, half_cols(h)], ALU.mult, ALU.mult
             )
+            nc.vector.scalar_tensor_tensor(u[h][:, t, :], y3[h][:, t, :], gs_t[:, col], sg[h][:, t, :], ALU.mult, ALU.mult)
 
         z_bf = [new(f"z_bf{h}", [P, HALF, PACK], BF16) for h in range(2)]
         z_w = [new(f"z_w{h}", [P, HALF], U32) for h in range(2)]
@@ -183,18 +202,28 @@ def tile_picked_cdswmxbemx_none_po_kernel(
                         stop=True,
                     )
 
-        def open_y(t):
+        def own_gate(t):
             col = slice(t, t + 1)
             nc.scalar.activation(own[t][:], y_ps[t][:], ACT.Sigmoid, bias=bias[:, col], scale=sl_t[:, col])
-            nc.scalar.copy(y_sb[t][:], y_ps[t][:])
 
+        own_gate(0)
+        nc.scalar.copy(y_sb[0][:], y_ps[0][:])
         for t in range(PACK):
-            open_y(t)
-            fetch_y(t, 0)
+            if t + 1 < PACK:
+                own_gate(t + 1)
+            fetch_sg(t, 0)
+            if t + 1 < PACK:
+                nc.scalar.copy(y_sb[t + 1][:], y_ps[t + 1][:])
+            fetch_y2(t, 0)
+        for t in range(PACK):
+            fetch_sg(t, 1)
+            fetch_y2(t, 1)
 
         fetch_y3(0, 0)
-        fetch_y3(1, 0)
+        cand_s = deal("cand_s", cand_s0, U8, 16)
         terms(0, 0)
+        fetch_y3(1, 0)
+        terms(1, 0)
         wb_w = new("wb_w", [P, S], U32)
         wb_s = new("wb_s", [P, S], U8)
         nc.vector.quantize_mx(wb_w[:].bitcast(FP8X4), wb_s[:], wb_bf[:].rearrange("p n t -> p (n t)"))
@@ -209,28 +238,22 @@ def tile_picked_cdswmxbemx_none_po_kernel(
                 start=True,
                 stop=True,
             )
-        bias2 = new("bias2", [P, PACK], F32)
-        nc.vector.scalar_tensor_tensor(bias2[:], sl2_t[:], -1.0, th2_t[:], ALU.mult, ALU.mult)
-        terms(1, 0)
-        fetch_y3(0, 1)
-        fetch_y3(1, 1)
+        nc.scalar.copy(b_sb[0][:], b_ps[0][:])
+        nc.scalar.copy(b_sb[1][:], b_ps[1][:])
         fetch_y3(2, 0)
         terms(2, 0)
-        fetch_y3(2, 1)
+        fetch_y3(0, 1)
         fetch_y3(3, 0)
         terms(3, 0)
-        fetch_y3(3, 1)
-        for t in range(PACK):
-            fetch_y(t, 1)
+        fetch_y3(1, 1)
         z_sum(0)
-        nc.vector.tensor_copy(b_sb[0][:], b_ps[0][:])
+        fetch_y3(2, 1)
         z_product(0)
-        nc.vector.tensor_copy(b_sb[1][:], b_ps[1][:])
+        fetch_y3(3, 1)
+        nc.vector.tensor_copy(b_sb[2][:], b_ps[2][:])
+        nc.vector.tensor_copy(b_sb[3][:], b_ps[3][:])
         for t in range(PACK):
             terms(t, 1)
-        nc.scalar.copy(b_sb[2][:], b_ps[2][:])
-        nc.scalar.copy(b_sb[3][:], b_ps[3][:])
-        z_sum(1)
 
         sg2, b5, q, dd, res = halves("sg2"), halves("b5"), halves("q"), halves("dd"), halves("res")
         res_bf = [new(f"res_bf{h}", [P, HALF, PACK], BF16) for h in range(2)]
@@ -246,30 +269,74 @@ def tile_picked_cdswmxbemx_none_po_kernel(
             )
             nc.scalar.activation(b5[h][:, t, :], b_sb[t][:].indirect(half_list(l_n5, h)), ACT.Copy)
 
-        def finish_pair(h, pair):
-            ts = slice(2 * pair, 2 * pair + 2)
-            t0, t1 = 2 * pair, 2 * pair + 1
-            nc.vector.tensor_tensor(dd[h][:, t0, :], b5[h][:, t0, :], b_sb[t0][:, half_cols(h)], ALU.subtract)
-            nc.vector.scalar_tensor_tensor(q[h][:, ts, :], a_ps[h, pair][:], 0.0625, sg2[h][:, ts, :], ALU.mult, ALU.mult)
-            nc.vector.tensor_tensor(dd[h][:, t1, :], b5[h][:, t1, :], b_sb[t1][:, half_cols(h)], ALU.subtract)
-            nc.vector.tensor_tensor(res[h][:, ts, :], q[h][:, ts, :], dd[h][:, ts, :], ALU.max)
-            nc.sync.dma_start(out_rows[:, ts, half_cols(h)], res[h][:, ts, :])
-
-        def planes(h):
-            nc.vector.tensor_copy(woven(res_bf[h][:]), planar(res[h][:]))
-            nc.vector.quantize_mx(
-                res_w[:, half_cols(h)].bitcast(FP8X4), res_s[:, half_cols(h)], res_bf[h][:].rearrange("p n t -> p (n t)")
-            )
-            nc.sync.dma_start(out_words[:, half_cols(h)], res_w[:, half_cols(h)].bitcast(I32))
-
         for h in range(2):
             for t in range(PACK):
                 fetch_b(t, h)
+
+        def pair_of(pair):
+            return slice(2 * pair, 2 * pair + 2)
+
+        def diff(t, h, c0=0, c1=HALF):
+            nc.vector.tensor_tensor(
+                dd[h][:, t, c0:c1], b5[h][:, t, c0:c1], b_sb[t][:, h * HALF + c0 : h * HALF + c1], ALU.subtract
+            )
+
+        def gated(h, pair):
+            ts = pair_of(pair)
+            nc.vector.scalar_tensor_tensor(q[h][:, ts, :], a_ps[h, pair][:], 0.0625, sg2[h][:, ts, :], ALU.mult, ALU.mult)
+
+        def larger(h, pair, c0=0, c1=HALF):
+            ts = pair_of(pair)
+            nc.vector.tensor_tensor(res[h][:, ts, c0:c1], q[h][:, ts, c0:c1], dd[h][:, ts, c0:c1], ALU.max)
+
+        def store_rows(h, pair):
+            nc.sync.dma_start(out_rows[:, pair_of(pair), half_cols(h)], res[h][:, pair_of(pair), :])
+
+        def round_res(h, c0=0, c1=HALF):
+            nc.vector.tensor_copy(woven(res_bf[h][:, c0:c1, :]), planar(res[h][:, :, c0:c1]))
+
+        def planes(h, c0=0, c1=HALF):
+            cols = slice(h * HALF + c0, h * HALF + c1)
+            nc.vector.quantize_mx(
+                res_w[:, cols].bitcast(FP8X4), res_s[:, cols], res_bf[h][:, c0:c1, :].rearrange("p n t -> p (n t)")
+            )
+
+        def store_words(h):
+            nc.sync.dma_start(out_words[:, half_cols(h)], res_w[:, half_cols(h)].bitcast(I32))
+
+        diff(0, 0)
+        z_sum(1)
+        gated(0, 0)
         z_product(1)
-        for h in range(2):
-            finish_pair(h, 0)
-            finish_pair(h, 1)
-            planes(h)
+        diff(1, 0)
+        diff(2, 0)
+        larger(0, 0)
+        store_rows(0, 0)
+        gated(0, 1)
+        diff(3, 0)
+        diff(0, 1)
+        larger(0, 1)
+        store_rows(0, 1)
+        gated(1, 0)
+        round_res(0)
+        diff(1, 1)
+        planes(0)
+        store_words(0)
+        larger(1, 0)
+        store_rows(1, 0)
+        diff(2, 1)
+        gated(1, 1)
+        quarters = [(0, HALF // 2), (HALF // 2, HALF)]
+        for c0, c1 in quarters:
+            diff(3, 1, c0, c1)
+        for c0, c1 in quarters:
+            larger(1, 1, c0, c1)
+        store_rows(1, 1)
+        for c0, c1 in quarters:
+            round_res(1, c0, c1)
+        for c0, c1 in quarters:
+            planes(1, c0, c1)
+        store_words(1)
         for qd in range(4):
-            queue = nc.scalar if qd % 2 else nc.sync
+            queue = nc.scalar if qd % 2 == 0 else nc.sync
             queue.dma_start(out_2[0][4 * qd : 4 * qd + 4, :].bitcast(I32), res_s[32 * qd : 32 * qd + 4, :].bitcast(I32))

@@ -99,83 +99,66 @@ def tile_picked_cdswmxbemx_none_po_kernel(
             w1s_d[:].rearrange("p (t m) -> p t m", t=PACK), w1s[:].rearrange("p (m t) -> p t m", t=PACK)
         )
         xq_w = new("xq_w", [P, S], U32)
-        nc.vector.tensor_copy(xq_w[:], xw[:].indirect(l_offs[:]))
+        for h in range(2):
+            nc.vector.tensor_copy(xq_w[:, half_cols(h)], xw[:].indirect(half_list(l_offs, h)))
 
         def neg_product(name, slope, threshold):
-            prod = new(name + "_prod", [P, PACK], F32)
             neg = new(name, [P, PACK], F32)
-            nc.gpsimd.tensor_tensor(prod[:], slope[:], threshold[:], ALU.mult)
-            nc.gpsimd.tensor_scalar(neg[:], prod[:], -1.0, 0.0, ALU.mult, ALU.add)
+            nc.vector.scalar_tensor_tensor(neg[:], slope[:], -1.0, threshold[:], ALU.mult, ALU.mult)
             return neg
 
         bias = neg_product("bias", sl_t, th_t)
 
         y_ps = [psum.tile([P, S], F32, name=f"y_ps{t}", tag=f"ya{t}") for t in range(PACK)]
         for t in range(PACK):
-            nc.tensor.matmul_mx(
-                y_ps[t][:],
-                lhsT=w1w_d[:, 2 * P * t : 2 * P * (t + 1)].bitcast(FP4X4),
-                lhsT_scale=w1s_d[:, P * t : P * (t + 1)],
-                rhs=xq_w[:].bitcast(FP8X4),
-                rhs_scale=xq_s[:],
-                start=True,
-                stop=True,
-            )
+            for h in range(2):
+                nc.tensor.matmul_mx(
+                    y_ps[t][:, half_cols(h)],
+                    lhsT=w1w_d[:, 2 * P * t : 2 * P * (t + 1)].bitcast(FP4X4),
+                    lhsT_scale=w1s_d[:, P * t : P * (t + 1)],
+                    rhs=xq_w[:, half_cols(h)].bitcast(FP8X4),
+                    rhs_scale=xq_s[:, half_cols(h)],
+                    start=True,
+                    stop=True,
+                )
 
-        def gather(name, window, lst, dtype):
-            t = new(name, [P, S], dtype)
-            nc.vector.tensor_copy(t[:], window[:].indirect(lst[:]))
-            return t
+        def pick_dealt(name, lst):
+            words = new(name + "_w", [P, S], U32)
+            scales = new(name + "_s", [P, S], U8)
+            for dst, window in ((words, xw), (scales, xs)):
+                nc.vector.tensor_copy(dst[:].rearrange("p (t m) -> p m t", t=PACK), window[:].indirect(lst[:]))
+            return words, scales
 
-        def deal(name, src, dtype, run):
-            t = new(name, [P, S], dtype)
-            nc.vector.tensor_copy(
-                t[:].rearrange("p (t c i) -> p c t i", t=PACK, i=run),
-                src[:].rearrange("p (c i t) -> p c t i", t=PACK, i=run),
-            )
-            return t
-
-        cb_w0 = gather("cb_w0", xw, l_cb, U32)
-        cb_s0 = gather("cb_s0", xs, l_cb, U8)
-        cb_w = deal("cb_w", cb_w0, U32, 4)
-        cand_w0 = gather("cand_w0", xw, l_cand, U32)
-        cb_s = deal("cb_s", cb_s0, U8, 16)
-        cand_s0 = gather("cand_s0", xs, l_cand, U8)
-        cand_w = deal("cand_w", cand_w0, U32, 4)
+        cb_w, cb_s = pick_dealt("cb", l_cb)
+        cand_w, cand_s = pick_dealt("cand", l_cand)
 
         wb_bf = new("wb_bf", [P, S, PACK], BF16)
         for c in range(4):
             cols = slice(c * P, (c + 1) * P)
             nc.gpsimd.tensor_scalar(woven(wb_bf[:, cols, :]), planar(wb_raw[:, :, cols]), 1.0, 0.0, ALU.mult, ALU.add)
 
-        bias2 = neg_product("bias2", sl2_t, th2_t)
-
         def halves(name, dtype=F32):
             return [new(f"{name}{h}", [P, PACK, HALF], dtype) for h in range(2)]
 
-        y_sb = [new(f"y_sb{t}", [P, S], F32) for t in range(PACK)]
+        y_own = [new(f"y_own{t}", [P, 2 * S], F32) for t in range(PACK)]
         b_sb = [new(f"b_sb{t}", [P, S], F32) for t in range(PACK)]
-        own = [new(f"own{t}", [P, S], F32) for t in range(PACK)]
-        sg, y2, y3, u, v = halves("sg"), halves("y2"), halves("y3"), halves("u"), halves("v")
+        sg, y2, y3, u, v = [new(name, [P, PACK, S], F32) for name in ("sg", "y2", "y3", "u", "v")]
 
-        def fetch_sg(t, h):
+        def fetch_sg(t):
             col = slice(t, t + 1)
-            nc.scalar.activation(
-                sg[h][:, t, :], y_sb[t][:].indirect(half_list(l_n1, h)), ACT.Sigmoid, bias=bias[:, col], scale=sl_t[:, col]
-            )
+            nc.scalar.activation(sg[:, t, :], y_own[t][:].indirect(l_n1[:]), ACT.Sigmoid, bias=bias[:, col], scale=sl_t[:, col])
 
-        def fetch_y2(t, h):
-            nc.scalar.activation(y2[h][:, t, :], y_sb[t][:].indirect(half_list(l_n2, h)), ACT.Copy)
+        def fetch_y2(t):
+            nc.scalar.activation(y2[:, t, :], y_own[t][:].indirect(l_n2[:]), ACT.Copy)
 
-        def fetch_y3(t, h):
-            nc.vector.tensor_copy(y3[h][:, t, :], y_sb[t][:].indirect(half_list(l_n3, h)))
+        def fetch_y3(t):
+            nc.vector.tensor_copy(y3[:, t, :], y_own[t][:].indirect(l_n3[:]))
 
-        def terms(t, h):
-            col = slice(t, t + 1)
-            nc.vector.scalar_tensor_tensor(
-                v[h][:, t, :], y2[h][:, t, :], gs_t[:, col], own[t][:, half_cols(h)], ALU.mult, ALU.mult
-            )
-            nc.vector.scalar_tensor_tensor(u[h][:, t, :], y3[h][:, t, :], gs_t[:, col], sg[h][:, t, :], ALU.mult, ALU.mult)
+        def term_u(t):
+            nc.vector.scalar_tensor_tensor(u[:, t, :], y3[:, t, :], gs_t[:, t : t + 1], sg[:, t, :], ALU.mult, ALU.mult)
+
+        def term_v(t):
+            nc.vector.scalar_tensor_tensor(v[:, t, :], y2[:, t, :], gs_t[:, t : t + 1], y_own[t][:, S:], ALU.mult, ALU.mult)
 
         z_bf = [new(f"z_bf{h}", [P, HALF, PACK], BF16) for h in range(2)]
         z_w = [new(f"z_w{h}", [P, HALF], U32) for h in range(2)]
@@ -183,7 +166,7 @@ def tile_picked_cdswmxbemx_none_po_kernel(
         a_ps = {}
 
         def z_sum(h):
-            nc.vector.tensor_tensor(woven(z_bf[h][:]), planar(u[h][:]), planar(v[h][:]), ALU.add)
+            nc.vector.tensor_tensor(woven(z_bf[h][:]), planar(u[:, :, half_cols(h)]), planar(v[:, :, half_cols(h)]), ALU.add)
 
         def z_product(h):
             nc.vector.quantize_mx(z_w[h][:].bitcast(FP8X4), z_s[h][:], z_bf[h][:].rearrange("p n t -> p (n t)"))
@@ -204,26 +187,26 @@ def tile_picked_cdswmxbemx_none_po_kernel(
 
         def own_gate(t):
             col = slice(t, t + 1)
-            nc.scalar.activation(own[t][:], y_ps[t][:], ACT.Sigmoid, bias=bias[:, col], scale=sl_t[:, col])
+            nc.scalar.activation(y_own[t][:, S:], y_ps[t][:], ACT.Sigmoid, bias=bias[:, col], scale=sl_t[:, col])
 
         own_gate(0)
-        nc.scalar.copy(y_sb[0][:], y_ps[0][:])
+        nc.scalar.copy(y_own[0][:, :S], y_ps[0][:])
         for t in range(PACK):
             if t + 1 < PACK:
                 own_gate(t + 1)
-            fetch_sg(t, 0)
+            fetch_sg(t)
             if t + 1 < PACK:
-                nc.scalar.copy(y_sb[t + 1][:], y_ps[t + 1][:])
-            fetch_y2(t, 0)
-        for t in range(PACK):
-            fetch_sg(t, 1)
-            fetch_y2(t, 1)
+                nc.scalar.copy(y_own[t + 1][:, :S], y_ps[t + 1][:])
+            fetch_y2(t)
 
-        fetch_y3(0, 0)
-        cand_s = deal("cand_s", cand_s0, U8, 16)
-        terms(0, 0)
-        fetch_y3(1, 0)
-        terms(1, 0)
+        fetch_y3(0)
+        term_v(0)
+        term_u(0)
+        fetch_y3(1)
+        bias2 = neg_product("bias2", sl2_t, th2_t)
+        term_u(1)
+        term_v(1)
+        fetch_y3(2)
         wb_w = new("wb_w", [P, S], U32)
         wb_s = new("wb_s", [P, S], U8)
         nc.vector.quantize_mx(wb_w[:].bitcast(FP8X4), wb_s[:], wb_bf[:].rearrange("p n t -> p (n t)"))
@@ -240,20 +223,16 @@ def tile_picked_cdswmxbemx_none_po_kernel(
             )
         nc.scalar.copy(b_sb[0][:], b_ps[0][:])
         nc.scalar.copy(b_sb[1][:], b_ps[1][:])
-        fetch_y3(2, 0)
-        terms(2, 0)
-        fetch_y3(0, 1)
-        fetch_y3(3, 0)
-        terms(3, 0)
-        fetch_y3(1, 1)
-        z_sum(0)
-        fetch_y3(2, 1)
-        z_product(0)
-        fetch_y3(3, 1)
+        term_u(2)
+        term_v(2)
+        fetch_y3(3)
         nc.vector.tensor_copy(b_sb[2][:], b_ps[2][:])
+        term_u(3)
+        term_v(3)
         nc.vector.tensor_copy(b_sb[3][:], b_ps[3][:])
-        for t in range(PACK):
-            terms(t, 1)
+        z_sum(0)
+        z_sum(1)
+        z_product(0)
 
         sg2, b5, q, dd, res = halves("sg2"), halves("b5"), halves("q"), halves("dd"), halves("res")
         res_bf = [new(f"res_bf{h}", [P, HALF, PACK], BF16) for h in range(2)]
@@ -262,16 +241,25 @@ def tile_picked_cdswmxbemx_none_po_kernel(
         out_rows = out_0.rearrange("(p t) j -> p t j", t=PACK)
         out_words = out_1[0].rearrange("p n t -> p (n t)").bitcast(I32)
 
-        def fetch_b(t, h):
+        def fetch_sg2(t, h):
             col = slice(t, t + 1)
             nc.scalar.activation(
                 sg2[h][:, t, :], b_sb[t][:].indirect(half_list(l_n4, h)), ACT.Sigmoid, bias=bias2[:, col], scale=sl2_t[:, col]
             )
-            nc.scalar.activation(b5[h][:, t, :], b_sb[t][:].indirect(half_list(l_n5, h)), ACT.Copy)
 
-        for h in range(2):
-            for t in range(PACK):
-                fetch_b(t, h)
+        def fetch_b5(t, h, c0=0, c1=HALF):
+            entries = l_n5[:, (h * HALF + c0) // 16 : (h * HALF + c1) // 16]
+            nc.scalar.activation(b5[h][:, t, c0:c1], b_sb[t][:].indirect(entries), ACT.Copy)
+
+        quarters = [(0, HALF // 2), (HALF // 2, HALF)]
+        for h, t in [(0, 0), (0, 1), (0, 2), (0, 3), (1, 0), (1, 1)]:
+            fetch_sg2(t, h)
+            fetch_b5(t, h)
+        fetch_sg2(2, 1)
+        fetch_sg2(3, 1)
+        fetch_b5(2, 1)
+        for c0, c1 in quarters:
+            fetch_b5(3, 1, c0, c1)
 
         def pair_of(pair):
             return slice(2 * pair, 2 * pair + 2)
@@ -285,12 +273,11 @@ def tile_picked_cdswmxbemx_none_po_kernel(
             ts = pair_of(pair)
             nc.vector.scalar_tensor_tensor(q[h][:, ts, :], a_ps[h, pair][:], 0.0625, sg2[h][:, ts, :], ALU.mult, ALU.mult)
 
-        def larger(h, pair, c0=0, c1=HALF):
-            ts = pair_of(pair)
+        def larger(h, ts, c0=0, c1=HALF):
             nc.vector.tensor_tensor(res[h][:, ts, c0:c1], q[h][:, ts, c0:c1], dd[h][:, ts, c0:c1], ALU.max)
 
-        def store_rows(h, pair):
-            nc.sync.dma_start(out_rows[:, pair_of(pair), half_cols(h)], res[h][:, pair_of(pair), :])
+        def store_rows(h, ts):
+            nc.sync.dma_start(out_rows[:, ts, half_cols(h)], res[h][:, ts, :])
 
         def round_res(h, c0=0, c1=HALF):
             nc.vector.tensor_copy(woven(res_bf[h][:, c0:c1, :]), planar(res[h][:, :, c0:c1]))
@@ -305,33 +292,32 @@ def tile_picked_cdswmxbemx_none_po_kernel(
             nc.sync.dma_start(out_words[:, half_cols(h)], res_w[:, half_cols(h)].bitcast(I32))
 
         diff(0, 0)
-        z_sum(1)
-        gated(0, 0)
         z_product(1)
         diff(1, 0)
+        gated(0, 0)
         diff(2, 0)
-        larger(0, 0)
-        store_rows(0, 0)
+        larger(0, pair_of(0))
+        store_rows(0, pair_of(0))
         gated(0, 1)
         diff(3, 0)
         diff(0, 1)
-        larger(0, 1)
-        store_rows(0, 1)
+        larger(0, pair_of(1))
+        store_rows(0, pair_of(1))
         gated(1, 0)
         round_res(0)
         diff(1, 1)
         planes(0)
         store_words(0)
-        larger(1, 0)
-        store_rows(1, 0)
-        diff(2, 1)
+        larger(1, pair_of(0))
+        store_rows(1, pair_of(0))
         gated(1, 1)
-        quarters = [(0, HALF // 2), (HALF // 2, HALF)]
+        diff(2, 1)
+        diff(3, 1, *quarters[0])
+        larger(1, slice(2, 3))
+        diff(3, 1, *quarters[1])
         for c0, c1 in quarters:
-            diff(3, 1, c0, c1)
-        for c0, c1 in quarters:
-            larger(1, 1, c0, c1)
-        store_rows(1, 1)
+            larger(1, slice(3, 4), c0, c1)
+        store_rows(1, pair_of(1))
         for c0, c1 in quarters:
             round_res(1, c0, c1)
         for c0, c1 in quarters:

from contextlib import ExitStack

import concourse.mybir as mybir

K, T, S = 512, 2048, 512
FLOPS = 3 * 2 * K * S * S

F32 = mybir.dt.float32
BF16 = mybir.dt.bfloat16
I32 = mybir.dt.int32
U32 = mybir.dt.uint32
U16 = mybir.dt.uint16
U8 = mybir.dt.uint8
FP8X4 = mybir.dt.float8_e4m3fn_x4
FP4X4 = mybir.dt.float4_e2m1fn_x4
ALU = mybir.AluOpType
ACT = mybir.ActivationFunctionType

P = 128
PACK = 4
HALF = S // 2
LIST_COLS = S // 16


def tile_picked_cdswmxbemx_none_po_kernel(
    tc, x_words, x_scales, w1_words, w1_scales, sl, th, gs, wb, sl2, th2, offs, n1, n2, n3, cand, cb, n4, n5, out_0, out_1, out_2
):
    nc = tc.nc
    with ExitStack() as ctx:
        lists = ctx.enter_context(tc.tile_pool(name="lists", bufs=1))
        sb = ctx.enter_context(tc.tile_pool(name="sb", bufs=1))
        psum = ctx.enter_context(tc.psum_pool(name="psum", bufs=1))

        def new(name, shape, dtype):
            return sb.tile(shape, dtype, name=name, align_bytes=64)

        def load_list(name, src):
            t = lists.tile([P, LIST_COLS], U16, name=name)
            nc.sync.dma_start(t[:], src)
            return t

        def load_rows(name, src, queue):
            t = new(name, [P, PACK], F32)
            queue.dma_start(t[:], src.rearrange("(p t) o -> p (t o)", t=PACK))
            return t

        def load_scale_rows(dst, src, queues):
            for q in range(4):
                queues[q].dma_start(dst[32 * q : 32 * q + 4, :].bitcast(I32), src[4 * q : 4 * q + 4, :].bitcast(I32))

        def half_cols(h):
            return slice(h * HALF, (h + 1) * HALF)

        def half_list(lst, h):
            return lst[:, h * LIST_COLS // 2 : (h + 1) * LIST_COLS // 2]

        def woven(t):
            return t.rearrange("p (c i) t -> p c t i", i=4)

        def planar(t):
            return t.rearrange("p t (c i) -> p c t i", i=4)

        xs = new("xs", [P, T], U8)
        nc.gpsimd.memset(xs[:].bitcast(I32), 0)
        w1s = new("w1s", [P, S], U8)
        nc.gpsimd.memset(w1s[:].bitcast(I32), 0)

        l_offs = load_list("l_offs", offs)
        xw = new("xw", [P, T], U32)
        nc.sync.dma_start(xw[:].bitcast(I32), x_words[0].rearrange("p n t -> p (n t)").bitcast(I32))
        w1w = new("w1w", [P, 2 * S], U8)
        nc.scalar.dma_start(w1w[:].bitcast(I32), w1_words[0].bitcast(I32))
        load_scale_rows(xs, x_scales[0], [nc.scalar] * 4)
        load_scale_rows(w1s, w1_scales[0], [nc.scalar, nc.scalar, nc.gpsimd, nc.gpsimd])
        sl_t = load_rows("sl_t", sl, nc.sync)
        th_t = load_rows("th_t", th, nc.sync)
        l_cb = load_list("l_cb", cb)
        l_n1 = load_list("l_n1", n1)
        l_n2 = load_list("l_n2", n2)
        l_cand = load_list("l_cand", cand)
        wb_raw = new("wb_raw", [P, PACK, S], F32)
        nc.sync.dma_start(wb_raw[:], wb.rearrange("(p t) n -> p t n", t=PACK))
        l_n3 = load_list("l_n3", n3)
        gs_t = load_rows("gs_t", gs, nc.sync)
        sl2_t = load_rows("sl2_t", sl2, nc.sync)
        th2_t = load_rows("th2_t", th2, nc.sync)
        l_n4 = load_list("l_n4", n4)
        l_n5 = load_list("l_n5", n5)

        w1w_d = new("w1w_d", [P, 2 * S], U8)
        nc.scalar.copy(
            w1w_d[:].bitcast(U16).rearrange("p (t m) -> p t m", t=PACK),
            w1w[:].bitcast(U16).rearrange("p (m t) -> p t m", t=PACK),
        )
        xq_s = new("xq_s", [P, S], U8)
        nc.vector.tensor_copy(xq_s[:], xs[:].indirect(l_offs[:]))
        w1s_d = new("w1s_d", [P, S], U8)
        nc.vector.tensor_copy(
            w1s_d[:].rearrange("p (t m) -> p t m", t=PACK), w1s[:].rearrange("p (m t) -> p t m", t=PACK)
        )
        xq_w = new("xq_w", [P, S], U32)
        for h in range(2):
            nc.vector.tensor_copy(xq_w[:, half_cols(h)], xw[:].indirect(half_list(l_offs, h)))

        def neg_product(name, slope, threshold):
            neg = new(name, [P, PACK], F32)
            nc.vector.scalar_tensor_tensor(neg[:], slope[:], -1.0, threshold[:], ALU.mult, ALU.mult)
            return neg

        bias = neg_product("bias", sl_t, th_t)

        y_ps = [psum.tile([P, S], F32, name=f"y_ps{t}", tag=f"ya{t}") for t in range(PACK)]
        for t in range(PACK):
            for h in range(2):
                nc.tensor.matmul_mx(
                    y_ps[t][:, half_cols(h)],
                    lhsT=w1w_d[:, 2 * P * t : 2 * P * (t + 1)].bitcast(FP4X4),
                    lhsT_scale=w1s_d[:, P * t : P * (t + 1)],
                    rhs=xq_w[:, half_cols(h)].bitcast(FP8X4),
                    rhs_scale=xq_s[:, half_cols(h)],
                    start=True,
                    stop=True,
                )

        def pick_dealt(name, lst):
            words = new(name + "_w", [P, S], U32)
            scales = new(name + "_s", [P, S], U8)
            for dst, window in ((words, xw), (scales, xs)):
                nc.vector.tensor_copy(dst[:].rearrange("p (t m) -> p m t", t=PACK), window[:].indirect(lst[:]))
            return words, scales

        cb_w, cb_s = pick_dealt("cb", l_cb)
        cand_w, cand_s = pick_dealt("cand", l_cand)

        wb_bf = new("wb_bf", [P, S, PACK], BF16)
        for c in range(4):
            cols = slice(c * P, (c + 1) * P)
            nc.gpsimd.tensor_scalar(woven(wb_bf[:, cols, :]), planar(wb_raw[:, :, cols]), 1.0, 0.0, ALU.mult, ALU.add)

        def halves(name, dtype=F32):
            return [new(f"{name}{h}", [P, PACK, HALF], dtype) for h in range(2)]

        y_own = [new(f"y_own{t}", [P, 2 * S], F32) for t in range(PACK)]
        b_sb = [new(f"b_sb{t}", [P, S], F32) for t in range(PACK)]
        sg, y2, y3, u, v = [new(name, [P, PACK, S], F32) for name in ("sg", "y2", "y3", "u", "v")]

        def fetch_sg(t):
            col = slice(t, t + 1)
            nc.scalar.activation(sg[:, t, :], y_own[t][:].indirect(l_n1[:]), ACT.Sigmoid, bias=bias[:, col], scale=sl_t[:, col])

        def fetch_y2(t):
            nc.scalar.activation(y2[:, t, :], y_own[t][:].indirect(l_n2[:]), ACT.Copy)

        def fetch_y3(t):
            nc.vector.tensor_copy(y3[:, t, :], y_own[t][:].indirect(l_n3[:]))

        def term_u(t):
            nc.vector.scalar_tensor_tensor(u[:, t, :], y3[:, t, :], gs_t[:, t : t + 1], sg[:, t, :], ALU.mult, ALU.mult)

        def term_v(t):
            nc.vector.scalar_tensor_tensor(v[:, t, :], y2[:, t, :], gs_t[:, t : t + 1], y_own[t][:, S:], ALU.mult, ALU.mult)

        z_bf = [new(f"z_bf{h}", [P, HALF, PACK], BF16) for h in range(2)]
        z_w = [new(f"z_w{h}", [P, HALF], U32) for h in range(2)]
        z_s = [new(f"z_s{h}", [P, HALF], U8) for h in range(2)]
        a_ps = {}

        def z_sum(h):
            nc.vector.tensor_tensor(woven(z_bf[h][:]), planar(u[:, :, half_cols(h)]), planar(v[:, :, half_cols(h)]), ALU.add)

        def z_product(h):
            nc.vector.quantize_mx(z_w[h][:].bitcast(FP8X4), z_s[h][:], z_bf[h][:].rearrange("p n t -> p (n t)"))
            for pair in range(2):
                bank = psum.tile([P, 2, HALF], F32, name=f"a_ps{h}{pair}", tag=f"ya{2 * h + pair}")
                a_ps[h, pair] = bank
                for i in range(2):
                    t = 2 * pair + i
                    nc.tensor.matmul_mx(
                        bank[:, i, :],
                        lhsT=cand_w[:, P * t : P * (t + 1)].bitcast(FP8X4),
                        lhsT_scale=cand_s[:, P * t : P * (t + 1)],
                        rhs=z_w[h][:].bitcast(FP8X4),
                        rhs_scale=z_s[h][:],
                        start=True,
                        stop=True,
                    )

        def own_gate(t):
            col = slice(t, t + 1)
            nc.scalar.activation(y_own[t][:, S:], y_ps[t][:], ACT.Sigmoid, bias=bias[:, col], scale=sl_t[:, col])

        own_gate(0)
        nc.scalar.copy(y_own[0][:, :S], y_ps[0][:])
        for t in range(PACK):
            if t + 1 < PACK:
                own_gate(t + 1)
            fetch_sg(t)
            if t + 1 < PACK:
                nc.scalar.copy(y_own[t + 1][:, :S], y_ps[t + 1][:])
            fetch_y2(t)

        fetch_y3(0)
        term_v(0)
        term_u(0)
        fetch_y3(1)
        bias2 = neg_product("bias2", sl2_t, th2_t)
        term_u(1)
        term_v(1)
        fetch_y3(2)
        wb_w = new("wb_w", [P, S], U32)
        wb_s = new("wb_s", [P, S], U8)
        nc.vector.quantize_mx(wb_w[:].bitcast(FP8X4), wb_s[:], wb_bf[:].rearrange("p n t -> p (n t)"))
        b_ps = [psum.tile([P, S], F32, name=f"b_ps{t}", tag=f"b{t}") for t in range(PACK)]
        for t in range(PACK):
            nc.tensor.matmul_mx(
                b_ps[t][:],
                lhsT=cb_w[:, P * t : P * (t + 1)].bitcast(FP8X4),
                lhsT_scale=cb_s[:, P * t : P * (t + 1)],
                rhs=wb_w[:].bitcast(FP8X4),
                rhs_scale=wb_s[:],
                start=True,
                stop=True,
            )
        nc.scalar.copy(b_sb[0][:], b_ps[0][:])
        nc.scalar.copy(b_sb[1][:], b_ps[1][:])
        term_u(2)
        term_v(2)
        fetch_y3(3)
        nc.vector.tensor_copy(b_sb[2][:], b_ps[2][:])
        term_u(3)
        term_v(3)
        nc.vector.tensor_copy(b_sb[3][:], b_ps[3][:])
        z_sum(0)
        z_sum(1)
        z_product(0)

        sg2, b5, q, dd, res = halves("sg2"), halves("b5"), halves("q"), halves("dd"), halves("res")
        res_bf = [new(f"res_bf{h}", [P, HALF, PACK], BF16) for h in range(2)]
        res_w = new("res_w", [P, S], U32)
        res_s = new("res_s", [P, S], U8)
        out_rows = out_0.rearrange("(p t) j -> p t j", t=PACK)
        out_words = out_1[0].rearrange("p n t -> p (n t)").bitcast(I32)

        def fetch_sg2(t, h):
            col = slice(t, t + 1)
            nc.scalar.activation(
                sg2[h][:, t, :], b_sb[t][:].indirect(half_list(l_n4, h)), ACT.Sigmoid, bias=bias2[:, col], scale=sl2_t[:, col]
            )

        def fetch_b5(t, h, c0=0, c1=HALF):
            entries = l_n5[:, (h * HALF + c0) // 16 : (h * HALF + c1) // 16]
            nc.scalar.activation(b5[h][:, t, c0:c1], b_sb[t][:].indirect(entries), ACT.Copy)

        quarters = [(0, HALF // 2), (HALF // 2, HALF)]
        for h, t in [(0, 0), (0, 1), (0, 2), (0, 3), (1, 0), (1, 1)]:
            fetch_sg2(t, h)
            fetch_b5(t, h)
        fetch_sg2(2, 1)
        fetch_sg2(3, 1)
        fetch_b5(2, 1)
        for c0, c1 in quarters:
            fetch_b5(3, 1, c0, c1)

        def pair_of(pair):
            return slice(2 * pair, 2 * pair + 2)

        def diff(t, h, c0=0, c1=HALF):
            nc.vector.tensor_tensor(
                dd[h][:, t, c0:c1], b5[h][:, t, c0:c1], b_sb[t][:, h * HALF + c0 : h * HALF + c1], ALU.subtract
            )

        def gated(h, pair):
            ts = pair_of(pair)
            nc.vector.scalar_tensor_tensor(q[h][:, ts, :], a_ps[h, pair][:], 0.0625, sg2[h][:, ts, :], ALU.mult, ALU.mult)

        def larger(h, ts, c0=0, c1=HALF):
            nc.vector.tensor_tensor(res[h][:, ts, c0:c1], q[h][:, ts, c0:c1], dd[h][:, ts, c0:c1], ALU.max)

        def store_rows(h, ts):
            nc.sync.dma_start(out_rows[:, ts, half_cols(h)], res[h][:, ts, :])

        def round_res(h, c0=0, c1=HALF):
            nc.vector.tensor_copy(woven(res_bf[h][:, c0:c1, :]), planar(res[h][:, :, c0:c1]))

        def planes(h, c0=0, c1=HALF):
            cols = slice(h * HALF + c0, h * HALF + c1)
            nc.vector.quantize_mx(
                res_w[:, cols].bitcast(FP8X4), res_s[:, cols], res_bf[h][:, c0:c1, :].rearrange("p n t -> p (n t)")
            )

        def store_words(h):
            nc.sync.dma_start(out_words[:, half_cols(h)], res_w[:, half_cols(h)].bitcast(I32))

        diff(0, 0)
        z_product(1)
        diff(1, 0)
        gated(0, 0)
        diff(2, 0)
        larger(0, pair_of(0))
        store_rows(0, pair_of(0))
        gated(0, 1)
        diff(3, 0)
        diff(0, 1)
        larger(0, pair_of(1))
        store_rows(0, pair_of(1))
        gated(1, 0)
        round_res(0)
        diff(1, 1)
        planes(0)
        store_words(0)
        larger(1, pair_of(0))
        store_rows(1, pair_of(0))
        gated(1, 1)
        diff(2, 1)
        diff(3, 1, *quarters[0])
        larger(1, slice(2, 3))
        diff(3, 1, *quarters[1])
        for c0, c1 in quarters:
            larger(1, slice(3, 4), c0, c1)
        store_rows(1, pair_of(1))
        for c0, c1 in quarters:
            round_res(1, c0, c1)
        for c0, c1 in quarters:
            planes(1, c0, c1)
        store_words(1)
        for qd in range(4):
            queue = nc.scalar if qd % 2 == 0 else nc.sync
            queue.dma_start(out_2[0][4 * qd : 4 * qd + 4, :].bitcast(I32), res_s[32 * qd : 32 * qd + 4, :].bitcast(I32))
